import numpy as np
import ml_dtypes

BF16 = ml_dtypes.bfloat16


def bf(x):
    return np.asarray(x, np.float32).astype(BF16)


def f32(x):
    return np.asarray(x, np.float32)


def f64(x):
    return np.asarray(x).astype(np.float64)


def striped(idx):
    return np.tile(idx.reshape(-1, 16).T, (8, 1))


S, K, H, M, N, E, Q = 256, 128, 256, 512, 128, 1, 128


def sigmoid(v):
    return 1.0 / (1.0 + np.exp(-v))


def setup_inputs():
    return {"base": bf(np.random.standard_normal((M, S))), "x": bf(np.random.standard_normal((K, N))), "w": bf(np.random.standard_normal((E, K, H)) / np.sqrt(K)), "b": f32(0.5 * np.random.standard_normal((H, E))), "w2": bf(1.5 * np.random.standard_normal((E, H, M)) / np.sqrt(H)), "offs": striped(np.random.permutation(S)[:N])}


def reference(base, x, w, b, w2, offs):
    idx = offs[:16].T.reshape(-1)
    z = f64(base).copy()
    for e in range(E):
        t = f64(w)[e].T @ f64(x)[:, e * Q : (e + 1) * Q] + f64(b)[:, e : e + 1]
        t = t * sigmoid(t)
        z[:, idx[e * Q : (e + 1) * Q]] += f64(w2)[e].T @ t
    return z

@@ -1,0 +1,75 @@
+import concourse.mybir as mybir
+from concourse.masks import make_identity
+
+P = 128
+BF16, F32, U16 = mybir.dt.bfloat16, mybir.dt.float32, mybir.dt.uint16
+SILU = mybir.ActivationFunctionType.Silu
+
+FLOPS = 2 * 128 * 256 * 128 + 2 * 256 * 512 * 128
+
+
+def tile_rows_ffnback_silu_kernel(tc, base, x, w, b, w2, offs, out):
+    nc = tc.nc
+    features, tokens = base.shape
+    entries = x.shape[1]
+    hidden = w.shape[2]
+    windows = features // P
+    blocks = hidden // P
+
+    with (
+        tc.tile_pool(name="held", bufs=1) as held,
+        tc.psum_pool(name="psum", bufs=1) as psum,
+    ):
+        ident = held.tile([P, P], BF16)
+        make_identity(nc, ident[:])
+
+        zeros = held.tile([P, 1], F32)
+        nc.vector.memset(zeros[:], 0.0)
+        silu_of_zeros = held.tile([P, 1], F32)
+        nc.scalar.activation(silu_of_zeros[:], zeros[:], SILU)
+
+        x_tile = held.tile([P, entries], BF16)
+        w_tile = held.tile([P, hidden], BF16)
+        base_tile = held.tile([P, windows, tokens], BF16)
+        offsets = held.tile([P, entries // 16], U16)
+        w2_tile = held.tile([P, blocks, features], BF16)
+        b_tile = held.tile([P, blocks], F32)
+        nc.sync.dma_start(x_tile[:], x)
+        nc.sync.dma_start(w_tile[:], w[0])
+        nc.scalar.dma_start(b_tile[:], b.rearrange("(a p) o -> p (a o)", p=P))
+        nc.sync.dma_start(base_tile[:], base.rearrange("(c p) s -> p c s", p=P))
+        nc.sync.dma_start(offsets[:], offs)
+        nc.sync.dma_start(w2_tile[:], w2[0].rearrange("(a p) m -> p a m", p=P))
+
+        h_tiles = []
+        for a in range(blocks):
+            pre = psum.tile([P, entries], F32, name=f"pre{a}")
+            nc.tensor.matmul(pre[:], w_tile[:, a * P : (a + 1) * P], x_tile[:], start=True, stop=True)
+            h = held.tile([P, entries], BF16, name=f"h{a}")
+            nc.scalar.activation(h[:], pre[:], SILU, bias=b_tile[:, a : a + 1])
+            h_tiles.append(h)
+
+        window_tiles = []
+        for c in range(windows):
+            window = psum.tile([P, tokens], F32, name=f"window{c}")
+            nc.tensor.matmul(window[:], ident[:], base_tile[:, c, :], start=True, stop=False)
+            window_tiles.append(window)
+
+        for a in range(blocks):
+            for c in range(windows):
+                nc.tensor.matmul(
+                    window_tiles[c][:].indirect(offsets[:]),
+                    w2_tile[:, a, c * P : (c + 1) * P],
+                    h_tiles[a][:],
+                    start=False,
+                    stop=(a == blocks - 1),
+                )
+
+        out_rows = out.rearrange("(c p) s -> p c s", p=P)
+        for c in range(windows):
+            z = held.tile([P, tokens], F32, name=f"z{c}")
+            if c % 2 == 0:
+                nc.vector.tensor_copy(z[:], window_tiles[c][:])
+            else:
+                nc.scalar.copy(z[:], window_tiles[c][:])
+            nc.sync.dma_start(out_rows[:, c, :], z[:])

@@ -36,15 +36,15 @@ def tile_rows_ffnback_silu_kernel(tc, base, x, w, b, w2, offs, out):
         b_tile = held.tile([P, blocks], F32)
         nc.sync.dma_start(x_tile[:], x)
         nc.sync.dma_start(w_tile[:], w[0])
-        nc.scalar.dma_start(b_tile[:], b.rearrange("(a p) o -> p (a o)", p=P))
-        nc.sync.dma_start(base_tile[:], base.rearrange("(c p) s -> p c s", p=P))
+        nc.scalar.dma_start(b_tile[:], b.rearrange("(p a) o -> p (a o)", p=P))
+        nc.sync.dma_start(base_tile[:], base.rearrange("(p c) s -> p c s", p=P))
         nc.sync.dma_start(offsets[:], offs)
-        nc.sync.dma_start(w2_tile[:], w2[0].rearrange("(a p) m -> p a m", p=P))
+        nc.sync.dma_start(w2_tile[:], w2[0].rearrange("(p a) m -> p a m", p=P))
 
         h_tiles = []
         for a in range(blocks):
             pre = psum.tile([P, entries], F32, name=f"pre{a}")
-            nc.tensor.matmul(pre[:], w_tile[:, a * P : (a + 1) * P], x_tile[:], start=True, stop=True)
+            nc.tensor.matmul(pre[:], w_tile[:, a::blocks], x_tile[:], start=True, stop=True)
             h = held.tile([P, entries], BF16, name=f"h{a}")
             nc.scalar.activation(h[:], pre[:], SILU, bias=b_tile[:, a : a + 1])
             h_tiles.append(h)
@@ -59,13 +59,13 @@ def tile_rows_ffnback_silu_kernel(tc, base, x, w, b, w2, offs, out):
             for c in range(windows):
                 nc.tensor.matmul(
                     window_tiles[c][:].indirect(offsets[:]),
-                    w2_tile[:, a, c * P : (c + 1) * P],
+                    w2_tile[:, a, c::windows],
                     h_tiles[a][:],
                     start=False,
                     stop=(a == blocks - 1),
                 )
 
-        out_rows = out.rearrange("(c p) s -> p c s", p=P)
+        out_rows = out.rearrange("(p c) s -> p c s", p=P)
         for c in range(windows):
             z = held.tile([P, tokens], F32, name=f"z{c}")
             if c % 2 == 0:

@@ -28,6 +28,12 @@ def tile_rows_ffnback_silu_kernel(tc, base, x, w, b, w2, offs, out):
         silu_of_zeros = held.tile([P, 1], F32)
         nc.scalar.activation(silu_of_zeros[:], zeros[:], SILU)
 
+        warm_up = held.tile([P, 512], BF16)
+        nc.vector.memset(warm_up[:], 0.0)
+        unread = psum.tile([P, 512], F32)
+        for turn in range(4):
+            nc.tensor.matmul(unread[:], warm_up[:, :P], warm_up[:], start=True, stop=True)
+
         x_tile = held.tile([P, entries], BF16)
         w_tile = held.tile([P, hidden], BF16)
         base_tile = held.tile([P, windows, tokens], BF16)

@@ -20,20 +20,6 @@ def tile_rows_ffnback_silu_kernel(tc, base, x, w, b, w2, offs, out):
         tc.tile_pool(name="held", bufs=1) as held,
         tc.psum_pool(name="psum", bufs=1) as psum,
     ):
-        ident = held.tile([P, P], BF16)
-        make_identity(nc, ident[:])
-
-        zeros = held.tile([P, 1], F32)
-        nc.vector.memset(zeros[:], 0.0)
-        silu_of_zeros = held.tile([P, 1], F32)
-        nc.scalar.activation(silu_of_zeros[:], zeros[:], SILU)
-
-        warm_up = held.tile([P, 512], BF16)
-        nc.vector.memset(warm_up[:], 0.0)
-        unread = psum.tile([P, 512], F32)
-        for turn in range(4):
-            nc.tensor.matmul(unread[:], warm_up[:, :P], warm_up[:], start=True, stop=True)
-
         x_tile = held.tile([P, entries], BF16)
         w_tile = held.tile([P, hidden], BF16)
         base_tile = held.tile([P, windows, tokens], BF16)
@@ -46,6 +32,20 @@ def tile_rows_ffnback_silu_kernel(tc, base, x, w, b, w2, offs, out):
         nc.sync.dma_start(base_tile[:], base.rearrange("(p c) s -> p c s", p=P))
         nc.sync.dma_start(offsets[:], offs)
         nc.sync.dma_start(w2_tile[:], w2[0].rearrange("(p a) m -> p a m", p=P))
+
+        warm_up = held.tile([P, 512], BF16)
+        nc.gpsimd.memset(warm_up[:], 0.0)
+        unread = psum.tile([P, 512], F32)
+        for turn in range(4):
+            nc.tensor.matmul(unread[:], warm_up[:, :P], warm_up[:], start=True, stop=True)
+
+        ident = held.tile([P, P], BF16)
+        make_identity(nc, ident[:])
+
+        zeros = held.tile([P, 1], F32)
+        nc.vector.memset(zeros[:], 0.0)
+        silu_of_zeros = held.tile([P, 1], F32)
+        nc.scalar.activation(silu_of_zeros[:], zeros[:], SILU)
 
         h_tiles = []
         for a in range(blocks):
@@ -61,8 +61,8 @@ def tile_rows_ffnback_silu_kernel(tc, base, x, w, b, w2, offs, out):
             nc.tensor.matmul(window[:], ident[:], base_tile[:, c, :], start=True, stop=False)
             window_tiles.append(window)
 
-        for a in range(blocks):
-            for c in range(windows):
+        for c in range(windows):
+            for a in range(blocks):
                 nc.tensor.matmul(
                     window_tiles[c][:].indirect(offsets[:]),
                     w2_tile[:, a, c::windows],
@@ -75,7 +75,7 @@ def tile_rows_ffnback_silu_kernel(tc, base, x, w, b, w2, offs, out):
         for c in range(windows):
             z = held.tile([P, tokens], F32, name=f"z{c}")
             if c % 2 == 0:
-                nc.vector.tensor_copy(z[:], window_tiles[c][:])
-            else:
                 nc.scalar.copy(z[:], window_tiles[c][:])
+            else:
+                nc.vector.tensor_copy(z[:], window_tiles[c][:])
             nc.sync.dma_start(out_rows[:, c, :], z[:])

@@ -13,8 +13,10 @@ def tile_rows_ffnback_silu_kernel(tc, base, x, w, b, w2, offs, out):
     features, tokens = base.shape
     entries = x.shape[1]
     hidden = w.shape[2]
-    windows = features // P
     blocks = hidden // P
+    halves = 2
+    half = features // halves
+    windows = half // P
 
     with (
         tc.tile_pool(name="held", bufs=1) as held,
@@ -22,16 +24,19 @@ def tile_rows_ffnback_silu_kernel(tc, base, x, w, b, w2, offs, out):
     ):
         x_tile = held.tile([P, entries], BF16)
         w_tile = held.tile([P, hidden], BF16)
-        base_tile = held.tile([P, windows, tokens], BF16)
-        offsets = held.tile([P, entries // 16], U16)
-        w2_tile = held.tile([P, blocks, features], BF16)
         b_tile = held.tile([P, blocks], F32)
+        base_tile = held.tile([P, halves, windows, tokens], BF16)
+        offsets = held.tile([P, entries // 16], U16)
         nc.sync.dma_start(x_tile[:], x)
         nc.sync.dma_start(w_tile[:], w[0])
         nc.scalar.dma_start(b_tile[:], b.rearrange("(p a) o -> p (a o)", p=P))
-        nc.sync.dma_start(base_tile[:], base.rearrange("(p c) s -> p c s", p=P))
+        nc.sync.dma_start(base_tile[:], base.rearrange("(g p c) s -> p g c s", g=halves, p=P))
         nc.sync.dma_start(offsets[:], offs)
-        nc.sync.dma_start(w2_tile[:], w2[0].rearrange("(p a) m -> p a m", p=P))
+        w2_tiles = []
+        for g in range(halves):
+            w2_half = held.tile([P, blocks, half], BF16, name=f"w2_half{g}")
+            nc.sync.dma_start(w2_half[:], w2[0, :, g * half : (g + 1) * half].rearrange("(p a) m -> p a m", p=P))
+            w2_tiles.append(w2_half)
 
         warm_up = held.tile([P, 512], BF16)
         nc.gpsimd.memset(warm_up[:], 0.0)
@@ -55,27 +60,30 @@ def tile_rows_ffnback_silu_kernel(tc, base, x, w, b, w2, offs, out):
             nc.scalar.activation(h[:], pre[:], SILU, bias=b_tile[:, a : a + 1])
             h_tiles.append(h)
 
-        window_tiles = []
-        for c in range(windows):
-            window = psum.tile([P, tokens], F32, name=f"window{c}")
-            nc.tensor.matmul(window[:], ident[:], base_tile[:, c, :], start=True, stop=False)
-            window_tiles.append(window)
+        window_tiles = {}
+        for g in range(halves):
+            for c in range(windows):
+                window = psum.tile([P, tokens], F32, name=f"window{g}{c}")
+                nc.tensor.matmul(window[:], ident[:], base_tile[:, g, c, :], start=True, stop=False)
+                window_tiles[g, c] = window
 
-        for c in range(windows):
-            for a in range(blocks):
-                nc.tensor.matmul(
-                    window_tiles[c][:].indirect(offsets[:]),
-                    w2_tile[:, a, c::windows],
-                    h_tiles[a][:],
-                    start=False,
-                    stop=(a == blocks - 1),
-                )
+        for g in range(halves):
+            for c in range(windows):
+                for a in range(blocks):
+                    nc.tensor.matmul(
+                        window_tiles[g, c][:].indirect(offsets[:]),
+                        w2_tiles[g][:, a, c::windows],
+                        h_tiles[a][:],
+                        start=False,
+                        stop=(a == blocks - 1),
+                    )
 
-        out_rows = out.rearrange("(p c) s -> p c s", p=P)
-        for c in range(windows):
-            z = held.tile([P, tokens], F32, name=f"z{c}")
-            if c % 2 == 0:
-                nc.scalar.copy(z[:], window_tiles[c][:])
-            else:
-                nc.vector.tensor_copy(z[:], window_tiles[c][:])
-            nc.sync.dma_start(out_rows[:, c, :], z[:])
+        out_rows = out.rearrange("(g p c) s -> g p c s", g=halves, p=P)
+        for g in range(halves):
+            for c in range(windows):
+                z = held.tile([P, tokens], F32, name=f"z{g}{c}")
+                if c == 0:
+                    nc.scalar.copy(z[:], window_tiles[g, c][:])
+                else:
+                    nc.vector.tensor_copy(z[:], window_tiles[g, c][:])
+                nc.sync.dma_start(out_rows[g, :, c, :], z[:])

import concourse.mybir as mybir
from concourse.masks import make_identity

P = 128
BF16, F32, U16 = mybir.dt.bfloat16, mybir.dt.float32, mybir.dt.uint16
SILU = mybir.ActivationFunctionType.Silu

FLOPS = 2 * 128 * 256 * 128 + 2 * 256 * 512 * 128


def tile_rows_ffnback_silu_kernel(tc, base, x, w, b, w2, offs, out):
    nc = tc.nc
    features, tokens = base.shape
    entries = x.shape[1]
    hidden = w.shape[2]
    blocks = hidden // P
    halves = 2
    half = features // halves
    windows = half // P

    with (
        tc.tile_pool(name="held", bufs=1) as held,
        tc.psum_pool(name="psum", bufs=1) as psum,
    ):
        x_tile = held.tile([P, entries], BF16)
        w_tile = held.tile([P, hidden], BF16)
        b_tile = held.tile([P, blocks], F32)
        base_tile = held.tile([P, halves, windows, tokens], BF16)
        offsets = held.tile([P, entries // 16], U16)
        nc.sync.dma_start(x_tile[:], x)
        nc.sync.dma_start(w_tile[:], w[0])
        nc.scalar.dma_start(b_tile[:], b.rearrange("(p a) o -> p (a o)", p=P))
        nc.sync.dma_start(base_tile[:], base.rearrange("(g p c) s -> p g c s", g=halves, p=P))
        nc.sync.dma_start(offsets[:], offs)
        w2_tiles = []
        for g in range(halves):
            w2_half = held.tile([P, blocks, half], BF16, name=f"w2_half{g}")
            nc.sync.dma_start(w2_half[:], w2[0, :, g * half : (g + 1) * half].rearrange("(p a) m -> p a m", p=P))
            w2_tiles.append(w2_half)

        warm_up = held.tile([P, 512], BF16)
        nc.gpsimd.memset(warm_up[:], 0.0)
        unread = psum.tile([P, 512], F32)
        for turn in range(4):
            nc.tensor.matmul(unread[:], warm_up[:, :P], warm_up[:], start=True, stop=True)

        ident = held.tile([P, P], BF16)
        make_identity(nc, ident[:])

        zeros = held.tile([P, 1], F32)
        nc.vector.memset(zeros[:], 0.0)
        silu_of_zeros = held.tile([P, 1], F32)
        nc.scalar.activation(silu_of_zeros[:], zeros[:], SILU)

        h_tiles = []
        for a in range(blocks):
            pre = psum.tile([P, entries], F32, name=f"pre{a}")
            nc.tensor.matmul(pre[:], w_tile[:, a::blocks], x_tile[:], start=True, stop=True)
            h = held.tile([P, entries], BF16, name=f"h{a}")
            nc.scalar.activation(h[:], pre[:], SILU, bias=b_tile[:, a : a + 1])
            h_tiles.append(h)

        window_tiles = {}
        for g in range(halves):
            for c in range(windows):
                window = psum.tile([P, tokens], F32, name=f"window{g}{c}")
                nc.tensor.matmul(window[:], ident[:], base_tile[:, g, c, :], start=True, stop=False)
                window_tiles[g, c] = window

        for g in range(halves):
            for c in range(windows):
                for a in range(blocks):
                    nc.tensor.matmul(
                        window_tiles[g, c][:].indirect(offsets[:]),
                        w2_tiles[g][:, a, c::windows],
                        h_tiles[a][:],
                        start=False,
                        stop=(a == blocks - 1),
                    )

        out_rows = out.rearrange("(g p c) s -> g p c s", g=halves, p=P)
        for g in range(halves):
            for c in range(windows):
                z = held.tile([P, tokens], F32, name=f"z{g}{c}")
                if c == 0:
                    nc.scalar.copy(z[:], window_tiles[g, c][:])
                else:
                    nc.vector.tensor_copy(z[:], window_tiles[g, c][:])
                nc.sync.dma_start(out_rows[g, :, c, :], z[:])
